import numpy as np
import ml_dtypes


def mxq(x, axis, fmt="e4m3"):
    dtype, down = {"e4m3": (ml_dtypes.float8_e4m3fn, 7), "e5m2": (ml_dtypes.float8_e5m2, 14)}[fmt]
    v = np.moveaxis(np.asarray(x, np.float32).astype(ml_dtypes.bfloat16).astype(np.float64), axis, -1)
    blocks = v.reshape(v.shape[:-1] + (-1, 32))
    amax = np.abs(blocks).max(-1, keepdims=True)
    byte = np.maximum(np.where(amax > 0, np.frexp(amax)[1] - 1 + 127, 0) - down, 1)
    scale = np.exp2(byte - 127.0)
    codes = (blocks / scale).astype(np.float32).astype(dtype).astype(np.float64)
    return np.moveaxis((codes * scale).reshape(v.shape), -1, axis)


WIDE = False


def mx_kscale(k):
    if not WIDE:
        return np.ones(k)
    levels = np.array([10, -10, 5, -5, 0])
    if k % 512:
        return np.exp2(np.random.permutation(np.resize(levels, k // 32))).repeat(32)
    a = np.empty((k // 512, 16))
    for p in range(k // 512):
        a[p, :8] = np.random.permutation(np.resize(levels, 8))
        for g in range(8):
            far = levels[np.abs(levels - a[p, g]) >= 10]
            a[p, g + 8] = far[np.random.randint(len(far))]
    return np.exp2(a.ravel()).repeat(32)


def f64(x):
    return np.asarray(x).astype(np.float64)


def striped(idx):
    return np.tile(np.asarray(idx).reshape(-1, 16).T, (8, 1)).astype(np.uint16)


def unstriped(offs):
    return offs[:16].T.reshape(-1).astype(np.int64)


E2M1 = np.array([0.0, 0.5, 1.0, 1.5, 2.0, 3.0, 4.0, 6.0, -0.0, -0.5, -1.0, -1.5, -2.0, -3.0, -4.0, -6.0])


def pack_weight(w, fmt):
    k, n = w.shape
    w = f64(np.asarray(w, np.float32).astype(ml_dtypes.bfloat16)).reshape(k // 32, 32, n)
    amax = np.abs(w).max(1)
    if fmt == "e4m3":
        byte = np.frexp(amax)[1] - 1 + 127 - 7
    else:
        mant, ex = np.frexp(amax / 6.0)
        byte = np.where(mant > 0.5, ex, ex - 1) + 127
    byte = np.clip(np.where(amax > 0, byte, 1), 1, 254)
    scaled = (w * np.exp2(127.0 - byte)[:, None, :]).reshape(k, n).astype(np.float32)
    by_word = np.ascontiguousarray(scaled.reshape(k // 512, 128, 4, n).transpose(0, 1, 3, 2))
    if fmt == "e4m3":
        words = by_word.astype(ml_dtypes.float8_e4m3fn).view(np.uint8)
    else:
        c = by_word.astype(ml_dtypes.float4_e2m1fn).view(np.uint8) & 0xF
        words = (c[..., 0::2] | (c[..., 1::2] << 4)).reshape(k // 512, 128, 2 * n)
    return np.ascontiguousarray(words), np.ascontiguousarray(byte.astype(np.uint8).reshape(k // 512, 16, n))


def unpack_weight(words, scales, fmt):
    g, _, n = scales.shape
    words = np.ascontiguousarray(words).reshape(g, 128, n, -1)
    if fmt == "e4m3":
        vals = words.view(ml_dtypes.float8_e4m3fn).astype(np.float64)
    else:
        nib = np.empty((g, 128, n, 4), np.uint8)
        nib[..., 0::2] = words & 0xF
        nib[..., 1::2] = words >> 4
        vals = E2M1[nib]
    vals = vals * np.repeat(np.exp2(scales.astype(np.float64) - 127.0), 8, axis=1)[..., None]
    return vals.transpose(0, 1, 3, 2).reshape(g * 512, n)


D, E, U, T, I, G, Q = 512, 512, 512, 2048, 512, 64, 128


def setup_inputs():
    n = np.random.standard_normal
    idx = np.random.permutation(T)[:I]
    idx2 = np.random.permutation(U)[:G]
    fd = mx_kscale(D)
    fe = mx_kscale(E)
    keysp = pack_weight(n((D, T)) / fd[:, None], "e2m1")
    valsp = pack_weight(n((E, T)) / fe[:, None], "e2m1")
    return {
        "pquery": (n((D, Q)) * 0.8 / np.sqrt(D) * fd[:, None]).astype(np.float32),
        "pgsum": (n((D, U)) / fd[:, None]).astype(np.float32),
        "query": (n((D, Q)) * 0.7 / np.sqrt(D) * fd[:, None]).astype(np.float32),
        "keys_words": keysp[0],
        "keys_scales": keysp[1],
        "gout": (n((E, Q)) * 1 / np.sqrt(E) * fe[:, None]).astype(np.float32),
        "pvals": (n((E, U)) * 0.7 / fe[:, None]).astype(np.float32),
        "vals_words": valsp[0],
        "vals_scales": valsp[1],
        "dpquery": (n((D, Q)) * 1.0 / np.sqrt(D) * fd[:, None]).astype(np.float32),
        "base": (0.5 * n((Q, U))).astype(np.float32),
        "offs": striped(idx),
        "offs2": striped(idx2),
    }


def reference(pquery, pgsum, query, keys_words, keys_scales, gout, pvals, vals_words, vals_scales, dpquery, base, offs, offs2):
    idx = unstriped(offs)
    idx2 = unstriped(offs2)
    keysu = unpack_weight(keys_words, keys_scales, "e2m1")
    valsu = unpack_weight(vals_words, vals_scales, "e2m1")
    pqueryq = mxq(f64(pquery), 0, "e4m3")
    pgsumq = mxq(f64(pgsum), 0, "e4m3")
    b = pqueryq.T @ pgsumq
    dpqueryq = mxq(f64(dpquery), 0, "e4m3")
    tb = dpqueryq.T @ pgsumq
    m1 = np.max(b, axis=1, keepdims=True)
    pb = np.exp(b - m1)
    z = np.sum(pb, axis=1, keepdims=True)
    queryq = mxq(f64(query), 0, "e4m3")
    keysidxg = keysu[:, idx]
    a = queryq.T @ keysidxg
    pa = np.exp(a)
    s = pa.reshape(Q, G, I // G).sum(axis=2)
    mo = np.exp(b[:, idx2] - m1)
    sh = mo / s
    sr = np.repeat(sh, I // G, axis=1)
    goutq = mxq(f64(gout), 0, "e4m3")
    pvalsq = mxq(f64(pvals), 0, "e4m3")
    c0 = goutq.T @ pvalsq
    valsidxg = valsu[:, idx]
    c1 = goutq.T @ valsidxg
    dsr = 1.0 / z * c1 * pa
    dsh = dsr.reshape(Q, G, I // G).sum(axis=2)
    dmo = 1.0 / z * (-1.0) * c0[:, idx2] + dsh / s
    dz = (np.sum(pb * c0, axis=1, keepdims=True) - np.sum(mo * c0[:, idx2], axis=1, keepdims=True) + np.sum(pa * sr * c1, axis=1, keepdims=True)) / np.square(z) * (-1.0)
    dpb = 1.0 / z * c0 + dz
    xpb = tb * pb
    xz = np.sum(xpb, axis=1, keepdims=True)
    xmo = tb[:, idx2] * mo
    xsh = xmo / s
    xsr = np.repeat(xsh, I // G, axis=1)
    xdsr = xz * 1.0 / np.square(z) * (-1.0) * c1 * pa
    xdsh = xdsr.reshape(Q, G, I // G).sum(axis=2)
    xdmo = xz * 1.0 / np.square(z) * (-1.0) * (-1.0) * c0[:, idx2] + xdsh / s
    xdz = (np.sum(xpb * c0, axis=1, keepdims=True) - np.sum(xmo * c0[:, idx2], axis=1, keepdims=True) + np.sum(xsr * pa * c1, axis=1, keepdims=True) - xz * z * 2.0 * (np.sum(pb * c0, axis=1, keepdims=True) - np.sum(mo * c0[:, idx2], axis=1, keepdims=True) + np.sum(pa * sr * c1, axis=1, keepdims=True)) / np.square(z)) / np.square(z) * (-1.0)
    xdpb = xz * 1.0 / np.square(z) * (-1.0) * c0 + xdz
    xe1 = xdmo * mo + xmo * dmo
    xs1 = np.zeros((Q, U))
    xs1[:, idx2] = xe1
    xdb = xdpb * pb + xpb * dpb + xs1
    y = xdb * 256.0 + f64(base)
    return y

@@ -1,0 +1,244 @@
+from contextlib import ExitStack
+
+import concourse.mybir as mybir
+from concourse.masks import make_identity
+
+D, E, U, T, I, G, Q = 512, 512, 512, 2048, 512, 64, 128
+FLOPS = 2 * 512 * 128 * 512 * 5
+
+F32 = mybir.dt.float32
+BF16 = mybir.dt.bfloat16
+I32 = mybir.dt.int32
+U32 = mybir.dt.uint32
+U16 = mybir.dt.uint16
+U8 = mybir.dt.uint8
+FP8X4 = mybir.dt.float8_e4m3fn_x4
+FP4X4 = mybir.dt.float4_e2m1fn_x4
+ALU = mybir.AluOpType
+ACT = mybir.ActivationFunctionType
+
+P = 128
+PACK = 4
+HALF = U // 2
+PAGE = I // G
+
+
+def tile_attend_hvopened_b_kernel(tc, pquery, pgsum, query, keys_words, keys_scales, gout, pvals,
+                                   vals_words, vals_scales, dpquery, base, offs, offs2, out):
+    nc = tc.nc
+    with ExitStack() as ctx:
+        sb = ctx.enter_context(tc.tile_pool(name="sb", bufs=1))
+        ps = ctx.enter_context(tc.psum_pool(name="ps", bufs=1))
+
+        def sbuf(name, shape, dtype=F32, tag=None):
+            return sb.tile(shape, dtype, name=name, tag=tag or name, align_bytes=64)
+
+        def column(name, tag=None):
+            return sbuf(name, [P, 1], tag=tag)
+
+        def load_rows(name, src, cols, queue):
+            raw = sbuf(name + "_raw", [P, PACK, cols.stop - cols.start])
+            queue.dma_start(out=raw[:], in_=src.rearrange("(p j) w -> p j w", j=PACK)[:, :, cols])
+            return raw
+
+        def interleave(name, raw, on_vector, tag=None):
+            width = raw.shape[2]
+            grouped = sbuf(name + "_bf", [P, width, PACK], BF16, tag=tag)
+            dst = grouped[:].rearrange("p (c i) t -> p c t i", i=4)
+            src = raw[:].rearrange("p t (c i) -> p c t i", i=4)
+            if on_vector:
+                nc.vector.tensor_copy(out=dst, in_=src)
+            else:
+                nc.scalar.copy(out=dst, in_=src)
+            return grouped
+
+        def planes(name, width):
+            return sbuf(name + "_codes", [P, width], U32), sbuf(name + "_scales", [P, width], U8)
+
+        def quantize(grouped, operand, cols):
+            codes, scales = operand
+            nc.vector.quantize_mx(out=codes[:, cols].bitcast(FP8X4), scales=scales[:, cols],
+                                  in_=grouped[:].rearrange("p w j -> p (w j)"))
+
+        def product(acc, rows, moving, cols, fmt):
+            nc.tensor.matmul_mx(out=acc, lhsT=rows[0][:].bitcast(FP8X4), lhsT_scale=rows[1][:],
+                                rhs=moving[0][:, cols].bitcast(fmt), rhs_scale=moving[1][:, cols],
+                                start=True, stop=True)
+
+        def load_scale_rows(tile, src, queue):
+            for r in range(4):
+                queue.dma_start(out=tile[r:P:32, :].bitcast(I32), in_=src[0][r:16:4, :].bitcast(I32))
+
+        rows_q = slice(0, Q)
+        whole = slice(0, U)
+        halves = [slice(0, HALF), slice(HALF, U)]
+
+        slots = sb.tile([P, I // 16], U16, name="slots")
+        opened = sb.tile([P, G // 16], U16, name="opened")
+        kw = sbuf("kw", [P, T], U16)
+        vw = sbuf("vw", [P, T], U16)
+        ks = sbuf("ks", [P, T], U8)
+        vs = sbuf("vs", [P, T], U8)
+        xs = sbuf("xs", [P, U])
+        ident = sbuf("ident", [P, P])
+        warm = column("warm")
+        warm2 = column("warm2")
+
+        nc.gpsimd.memset(ks[:].bitcast(I32), 0)
+        nc.vector.memset(warm[:], 0.0)
+        nc.vector.memset(vs[:].bitcast(I32), 0)
+        nc.scalar.activation(out=warm2[:], in_=warm[:], func=ACT.Exp)
+        nc.sync.dma_start(slots[:], offs)
+        load_scale_rows(ks, keys_scales, nc.sync)
+        nc.sync.dma_start(out=kw[:].bitcast(I32), in_=keys_words[0].bitcast(I32))
+        pq_raw = load_rows("pq", pquery, rows_q, nc.sync)
+        pg_raw = [load_rows("pg0", pgsum, halves[0], nc.sync)]
+        load_scale_rows(vs, vals_scales, nc.sync)
+        nc.sync.dma_start(out=vw[:].bitcast(I32), in_=vals_words[0].bitcast(I32))
+        q_raw = load_rows("q", query, rows_q, nc.sync)
+        go_raw = load_rows("go", gout, rows_q, nc.sync)
+        pg_raw.append(load_rows("pg1", pgsum, halves[1], nc.sync))
+        dq_raw = load_rows("dq", dpquery, rows_q, nc.sync)
+        nc.sync.dma_start(opened[:], offs2)
+        pv_raw = [load_rows("pv%d" % h, pvals, halves[h], nc.sync) for h in range(2)]
+        base_sb = sbuf("base_sb", [P, U])
+        nc.sync.dma_start(out=base_sb[:], in_=base)
+        make_identity(nc, ident[:])
+        nc.gpsimd.memset(xs[:], 0.0)
+
+        keys = (sbuf("keys_w", [P, I], U16), sbuf("keys_s", [P, I], U8))
+        vals = (sbuf("vals_w", [P, I], U16), sbuf("vals_s", [P, I], U8))
+        pq = planes("pq", Q)
+        dq = planes("dq", Q)
+        qq = planes("qq", Q)
+        go = planes("go", Q)
+        pg = planes("pg", U)
+        pv = planes("pv", U)
+
+        nc.vector.tensor_copy(keys[1][:], ks[:].indirect(slots[:]))
+        nc.vector.tensor_copy(keys[0][:], kw[:].indirect(slots[:]))
+        pq_bf = interleave("pq", pq_raw, False)
+        pg_bf0 = interleave("pg0", pg_raw[0], False)
+        nc.vector.tensor_copy(vals[1][:], vs[:].indirect(slots[:]))
+        quantize(pq_bf, pq, rows_q)
+        nc.vector.tensor_copy(vals[0][:], vw[:].indirect(slots[:]))
+        q_bf = interleave("q", q_raw, False)
+        go_bf = interleave("go", go_raw, False)
+        quantize(q_bf, qq, rows_q)
+        a_ps = ps.tile([P, I], F32, name="a_ps", tag="a")
+        product(a_ps[:], qq, keys, whole, FP4X4)
+        quantize(pg_bf0, pg, halves[0])
+        quantize(go_bf, go, rows_q)
+        c1_ps = ps.tile([P, I], F32, name="c1_ps", tag="c1")
+        product(c1_ps[:], go, vals, whole, FP4X4)
+        terms = sbuf("terms", [P, PAGE, 2 * G])
+        nc.scalar.activation(out=terms[:, :, :G], in_=a_ps[:].rearrange("p (g j) -> p j g", j=PAGE), func=ACT.Exp)
+        pg_bf1 = interleave("pg1", pg_raw[1], True)
+        dq_bf = interleave("dq", dq_raw, False)
+        quantize(pg_bf1, pg, halves[1])
+        b_ps = ps.tile([P, U], F32, name="b_ps")
+        product(b_ps[:], pq, pg, whole, FP8X4)
+        nc.vector.tensor_tensor(out=terms[:, :, G:], in0=c1_ps[:].rearrange("p (g j) -> p j g", j=PAGE),
+                                in1=terms[:, :, :G], op=ALU.mult)
+        quantize(dq_bf, dq, rows_q)
+        tb_ps = ps.tile([P, U], F32, name="tb_ps")
+        product(tb_ps[:], dq, pg, whole, FP8X4)
+        sums_t_ps = ps.tile([P, P], F32, name="sums_t_ps", tag="a")
+        for j in range(PAGE):
+            nc.tensor.matmul(sums_t_ps[:], lhsT=terms[:, j, :], rhs=ident[:], is_transpose=True,
+                             start=(j == 0), stop=(j == PAGE - 1))
+
+        b = sbuf("b", [P, U])
+        m = column("m", tag="late")
+        neg_m = column("neg_m")
+        nc.vector.tensor_scalar(out=b[:], in0=b_ps[:], scalar1=1.0, scalar2=None, op0=ALU.mult, op1=ALU.max,
+                                accum_out=m[:])
+        pv_bf0 = interleave("pv0", pv_raw[0], False)
+        nc.scalar.mul(neg_m[:], m[:], -1.0)
+        pb = sbuf("pb", [P, U])
+        z = column("z")
+        nc.scalar.activation(out=pb[:], in_=b[:], func=ACT.Exp, bias=neg_m[:], accum_out=z[:])
+        sums_t = sbuf("sums_t", [P, P])
+        nc.scalar.copy(out=sums_t[:], in_=sums_t_ps[:])
+        sums_ps = ps.tile([P, P], F32, name="sums_ps", tag="c1")
+        nc.tensor.transpose(sums_ps[:], sums_t[:], ident[:])
+        tb = sbuf("tb", [P, U])
+        nc.scalar.copy(out=tb[:], in_=tb_ps[:])
+        pv_bf1 = interleave("pv1", pv_raw[1], True, tag="late")
+        b_g = sbuf("b_g", [P, G])
+        nc.vector.tensor_copy(b_g[:], b[:].indirect(opened[:]))
+        r = column("r")
+        nc.vector.reciprocal(r[:], z[:])
+        c0_ps = ps.tile([P, U], F32, name="c0_ps")
+        c0_b_ps = ps.tile([P, HALF], F32, name="c0_b_ps")
+        c0 = sbuf("c0", [P, U])
+        quantize(pv_bf0, pv, halves[0])
+        product(c0_ps[:, halves[0]], go, pv, halves[0], FP8X4)
+        nc.scalar.copy(out=c0[:, halves[0]], in_=c0_ps[:, halves[0]])
+        quantize(pv_bf1, pv, halves[1])
+        product(c0_b_ps[:], go, pv, halves[1], FP8X4)
+        product(c0_ps[:, halves[1]], go, pv, halves[1], FP8X4)
+        nc.scalar.copy(out=c0[:, halves[1]], in_=c0_b_ps[:])
+        xpb = sbuf("xpb", [P, U])
+        xz = column("xz")
+        nc.vector.scalar_tensor_tensor(out=xpb[:], in0=tb_ps[:], scalar=1.0, in1=pb[:], op0=ALU.mult, op1=ALU.mult,
+                                       accum_out=xz[:])
+        rs = sbuf("rs", [P, G])
+        nc.vector.reciprocal(rs[:], sums_ps[:, :G])
+        tb_g = sbuf("tb_g", [P, G])
+        nc.vector.tensor_copy(tb_g[:], tb[:].indirect(opened[:]))
+        hh = sbuf("hh", [P, G])
+        nc.vector.tensor_tensor(out=hh[:], in0=sums_ps[:, G:], in1=rs[:], op=ALU.mult)
+
+        neg_gain = column("neg_gain")
+        neg_r = column("neg_r")
+        r_gain = column("r_gain")
+        mu = column("mu")
+        mo = sbuf("mo", [P, G])
+        mo_s = sbuf("mo_s", [P, G])
+        nc.scalar.mul(neg_gain[:], r[:], -256.0)
+        nc.scalar.activation(out=mo[:], in_=b_g[:], func=ACT.Exp, bias=neg_m[:])
+        nc.scalar.activation(out=mu[:], in_=xz[:], func=ACT.Copy, scale=r[:])
+        nc.scalar.activation(out=mo_s[:], in_=mo[:], func=ACT.Copy, scale=neg_gain[:])
+        nc.scalar.mul(neg_r[:], r[:], -1.0)
+        nc.scalar.activation(out=r_gain[:], in_=r[:], func=ACT.Copy, scale=neg_gain[:])
+
+        slope_g = sbuf("slope_g", [P, G])
+        nc.vector.scalar_tensor_tensor(out=slope_g[:], in0=tb_g[:], scalar=mu[:], in1=mo_s[:], op0=ALU.subtract,
+                                       op1=ALU.mult)
+        nd = sbuf("nd", [P, G])
+        nc.vector.tensor_tensor(out=nd[:], in0=c0[:].indirect(opened[:]), in1=hh[:], op=ALU.subtract)
+        y = sbuf("y", [P, U])
+        n0 = column("n0")
+        j1 = sbuf("j1", [P, G])
+        n1 = column("n1")
+        nc.vector.scalar_tensor_tensor(out=j1[:], in0=nd[:], scalar=1.0 / 256.0, in1=mo_s[:], op0=ALU.mult,
+                                       op1=ALU.mult, accum_out=n1[:])
+        nc.vector.tensor_tensor(out=xs[:].indirect(opened[:]), in0=nd[:], in1=slope_g[:], op=ALU.mult)
+        nc.vector.scalar_tensor_tensor(out=y[:], in0=c0_ps[:], scalar=1.0, in1=pb[:], op0=ALU.mult, op1=ALU.mult,
+                                       accum_out=n0[:])
+        bx = sbuf("bx", [P, U])
+        nc.gpsimd.tensor_tensor(out=bx[:], in0=xs[:], in1=base_sb[:], op=ALU.add)
+        j2 = sbuf("j2", [P, U])
+        k1 = column("k1")
+        nc.scalar.activation(out=j2[:], in_=xs[:], func=ACT.Copy, scale=neg_r[:], accum_out=k1[:])
+        n = column("n")
+        nc.scalar.activation(out=n[:], in_=n0[:], func=ACT.Identity, scale=r[:], bias=n1[:])
+        slope = sbuf("slope", [P, U])
+        nc.vector.scalar_tensor_tensor(out=slope[:], in0=tb_ps[:], scalar=mu[:], in1=pb[:], op0=ALU.subtract,
+                                       op1=ALU.mult)
+        u = sbuf("u", [P, U])
+        k0 = column("k0")
+        nc.vector.scalar_tensor_tensor(out=u[:], in0=c0_ps[:], scalar=n[:], in1=slope[:], op0=ALU.subtract,
+                                       op1=ALU.mult, accum_out=k0[:])
+        shift = column("shift")
+        nc.scalar.activation(out=shift[:], in_=k0[:], func=ACT.Identity, scale=r_gain[:], bias=k1[:])
+        w = [sbuf("w%d" % h, [P, HALF]) for h in range(2)]
+        result = [sbuf("result%d" % h, [P, HALF]) for h in range(2)]
+        for h in range(2):
+            nc.vector.scalar_tensor_tensor(out=w[h][:], in0=u[:, halves[h]], scalar=neg_gain[:],
+                                           in1=bx[:, halves[h]], op0=ALU.mult, op1=ALU.subtract)
+        for h in range(2):
+            nc.vector.scalar_tensor_tensor(out=result[h][:], in0=pb[:, halves[h]], scalar=shift[:],
+                                           in1=w[h][:], op0=ALU.mult, op1=ALU.subtract)
+            nc.sync.dma_start(out=out[:, halves[h]], in_=result[h][:])

@@ -16,6 +16,7 @@ FP8X4 = mybir.dt.float8_e4m3fn_x4
 FP4X4 = mybir.dt.float4_e2m1fn_x4
 ALU = mybir.AluOpType
 ACT = mybir.ActivationFunctionType
+AXIS = mybir.AxisListType
 
 P = 128
 PACK = 4
@@ -36,8 +37,8 @@ def tile_attend_hvopened_b_kernel(tc, pquery, pgsum, query, keys_words, keys_sca
         def column(name, tag=None):
             return sbuf(name, [P, 1], tag=tag)
 
-        def load_rows(name, src, cols, queue):
-            raw = sbuf(name + "_raw", [P, PACK, cols.stop - cols.start])
+        def load_rows(name, src, cols, queue, tag=None):
+            raw = sbuf(name + "_raw", [P, PACK, cols.stop - cols.start], tag=tag)
             queue.dma_start(out=raw[:], in_=src.rearrange("(p j) w -> p j w", j=PACK)[:, :, cols])
             return raw
 
@@ -52,8 +53,8 @@ def tile_attend_hvopened_b_kernel(tc, pquery, pgsum, query, keys_words, keys_sca
                 nc.scalar.copy(out=dst, in_=src)
             return grouped
 
-        def planes(name, width):
-            return sbuf(name + "_codes", [P, width], U32), sbuf(name + "_scales", [P, width], U8)
+        def planes(name, width, tag=None):
+            return sbuf(name + "_codes", [P, width], U32, tag=tag), sbuf(name + "_scales", [P, width], U8)
 
         def quantize(grouped, operand, cols):
             codes, scales = operand
@@ -83,154 +84,150 @@ def tile_attend_hvopened_b_kernel(tc, pquery, pgsum, query, keys_words, keys_sca
         ident = sbuf("ident", [P, P])
         warm = column("warm")
         warm2 = column("warm2")
-
         nc.gpsimd.memset(ks[:].bitcast(I32), 0)
         nc.vector.memset(warm[:], 0.0)
         nc.vector.memset(vs[:].bitcast(I32), 0)
         nc.scalar.activation(out=warm2[:], in_=warm[:], func=ACT.Exp)
         nc.sync.dma_start(slots[:], offs)
-        load_scale_rows(ks, keys_scales, nc.sync)
         nc.sync.dma_start(out=kw[:].bitcast(I32), in_=keys_words[0].bitcast(I32))
-        pq_raw = load_rows("pq", pquery, rows_q, nc.sync)
-        pg_raw = [load_rows("pg0", pgsum, halves[0], nc.sync)]
-        load_scale_rows(vs, vals_scales, nc.sync)
-        nc.sync.dma_start(out=vw[:].bitcast(I32), in_=vals_words[0].bitcast(I32))
+        load_scale_rows(ks, keys_scales, nc.sync)
         q_raw = load_rows("q", query, rows_q, nc.sync)
-        go_raw = load_rows("go", gout, rows_q, nc.sync)
-        pg_raw.append(load_rows("pg1", pgsum, halves[1], nc.sync))
+        pg0_raw = load_rows("pg0", pgsum, halves[0], nc.sync)
+        pq_raw = load_rows("pq", pquery, rows_q, nc.sync)
+        load_scale_rows(vs, vals_scales, nc.sync)
+        pg1_raw = load_rows("pg1", pgsum, halves[1], nc.sync, "pg1")
         dq_raw = load_rows("dq", dpquery, rows_q, nc.sync)
+        go_raw = load_rows("go", gout, rows_q, nc.sync)
+        nc.sync.dma_start(out=vw[:].bitcast(I32), in_=vals_words[0].bitcast(I32))
         nc.sync.dma_start(opened[:], offs2)
-        pv_raw = [load_rows("pv%d" % h, pvals, halves[h], nc.sync) for h in range(2)]
+        pv0_raw = load_rows("pv0", pvals, halves[0], nc.sync, "pv0")
+        pv1_raw = load_rows("pv1", pvals, halves[1], nc.sync, "pv1")
         base_sb = sbuf("base_sb", [P, U])
         nc.sync.dma_start(out=base_sb[:], in_=base)
         make_identity(nc, ident[:])
         nc.gpsimd.memset(xs[:], 0.0)
-
         keys = (sbuf("keys_w", [P, I], U16), sbuf("keys_s", [P, I], U8))
         vals = (sbuf("vals_w", [P, I], U16), sbuf("vals_s", [P, I], U8))
-        pq = planes("pq", Q)
         dq = planes("dq", Q)
         qq = planes("qq", Q)
         go = planes("go", Q)
-        pg = planes("pg", U)
+        page_planes = planes("pg", U + Q, "pg1")
+        pg = [x[:, :U] for x in page_planes]
+        pq = [x[:, U:] for x in page_planes]
         pv = planes("pv", U)
-
-        nc.vector.tensor_copy(keys[1][:], ks[:].indirect(slots[:]))
         nc.vector.tensor_copy(keys[0][:], kw[:].indirect(slots[:]))
-        pq_bf = interleave("pq", pq_raw, False)
-        pg_bf0 = interleave("pg0", pg_raw[0], False)
-        nc.vector.tensor_copy(vals[1][:], vs[:].indirect(slots[:]))
-        quantize(pq_bf, pq, rows_q)
-        nc.vector.tensor_copy(vals[0][:], vw[:].indirect(slots[:]))
+        nc.vector.tensor_copy(keys[1][:], ks[:].indirect(slots[:]))
         q_bf = interleave("q", q_raw, False)
-        go_bf = interleave("go", go_raw, False)
+        pg_bf0 = interleave("pg0", pg0_raw, False)
+        pq_bf = interleave("pq", pq_raw, False)
         quantize(q_bf, qq, rows_q)
         a_ps = ps.tile([P, I], F32, name="a_ps", tag="a")
         product(a_ps[:], qq, keys, whole, FP4X4)
-        quantize(pg_bf0, pg, halves[0])
-        quantize(go_bf, go, rows_q)
-        c1_ps = ps.tile([P, I], F32, name="c1_ps", tag="c1")
-        product(c1_ps[:], go, vals, whole, FP4X4)
+        nc.vector.tensor_copy(vals[1][:], vs[:].indirect(slots[:]))
         terms = sbuf("terms", [P, PAGE, 2 * G])
         nc.scalar.activation(out=terms[:, :, :G], in_=a_ps[:].rearrange("p (g j) -> p j g", j=PAGE), func=ACT.Exp)
-        pg_bf1 = interleave("pg1", pg_raw[1], True)
+        pg_bf1 = interleave("pg1", pg1_raw, True)
         dq_bf = interleave("dq", dq_raw, False)
+        go_bf = interleave("go", go_raw, False)
+        quantize(pg_bf0, pg, halves[0])
+        quantize(pq_bf, pq, rows_q)
         quantize(pg_bf1, pg, halves[1])
         b_ps = ps.tile([P, U], F32, name="b_ps")
         product(b_ps[:], pq, pg, whole, FP8X4)
-        nc.vector.tensor_tensor(out=terms[:, :, G:], in0=c1_ps[:].rearrange("p (g j) -> p j g", j=PAGE),
-                                in1=terms[:, :, :G], op=ALU.mult)
         quantize(dq_bf, dq, rows_q)
         tb_ps = ps.tile([P, U], F32, name="tb_ps")
         product(tb_ps[:], dq, pg, whole, FP8X4)
-        sums_t_ps = ps.tile([P, P], F32, name="sums_t_ps", tag="a")
-        for j in range(PAGE):
-            nc.tensor.matmul(sums_t_ps[:], lhsT=terms[:, j, :], rhs=ident[:], is_transpose=True,
-                             start=(j == 0), stop=(j == PAGE - 1))
-
+        quantize(go_bf, go, rows_q)
+        nc.vector.tensor_copy(vals[0][:], vw[:].indirect(slots[:]))
+        c1_ps = ps.tile([P, I], F32, name="c1_ps", tag="c1")
+        product(c1_ps[:], go, vals, whole, FP4X4)
         b = sbuf("b", [P, U])
-        m = column("m", tag="late")
+        nc.scalar.copy(out=b[:], in_=b_ps[:])
+        tb = sbuf("tb", [P, U])
+        nc.scalar.copy(out=tb[:], in_=tb_ps[:])
         neg_m = column("neg_m")
-        nc.vector.tensor_scalar(out=b[:], in0=b_ps[:], scalar1=1.0, scalar2=None, op0=ALU.mult, op1=ALU.max,
-                                accum_out=m[:])
-        pv_bf0 = interleave("pv0", pv_raw[0], False)
-        nc.scalar.mul(neg_m[:], m[:], -1.0)
+        nc.vector.tensor_reduce(out=neg_m[:], in_=b_ps[:], axis=AXIS.X, op=ALU.max, negate=True)
+        b_g = sbuf("b_g", [P, G])
+        nc.vector.tensor_copy(b_g[:], b[:].indirect(opened[:]))
+        tb_g = sbuf("tb_g", [P, G])
+        nc.vector.tensor_copy(tb_g[:], tb[:].indirect(opened[:]))
+        sums_t_ps = ps.tile([P, P], F32, name="sums_t_ps", tag="a")
+        for part in range(2):
+            places = slice(part * PAGE // 2, (part + 1) * PAGE // 2)
+            nc.vector.tensor_tensor(out=terms[:, places, G:],
+                                    in0=c1_ps[:].rearrange("p (g j) -> p j g", j=PAGE)[:, places, :],
+                                    in1=terms[:, places, :G], op=ALU.mult)
+            for j in range(places.start, places.stop):
+                nc.tensor.matmul(sums_t_ps[:], lhsT=terms[:, j, :], rhs=ident[:], is_transpose=True,
+                                 start=(j == 0), stop=(j == PAGE - 1))
         pb = sbuf("pb", [P, U])
         z = column("z")
         nc.scalar.activation(out=pb[:], in_=b[:], func=ACT.Exp, bias=neg_m[:], accum_out=z[:])
-        sums_t = sbuf("sums_t", [P, P])
-        nc.scalar.copy(out=sums_t[:], in_=sums_t_ps[:])
-        sums_ps = ps.tile([P, P], F32, name="sums_ps", tag="c1")
-        nc.tensor.transpose(sums_ps[:], sums_t[:], ident[:])
-        tb = sbuf("tb", [P, U])
-        nc.scalar.copy(out=tb[:], in_=tb_ps[:])
-        pv_bf1 = interleave("pv1", pv_raw[1], True, tag="late")
-        b_g = sbuf("b_g", [P, G])
-        nc.vector.tensor_copy(b_g[:], b[:].indirect(opened[:]))
+        mo = sbuf("mo", [P, G])
+        nc.scalar.activation(out=mo[:], in_=b_g[:], func=ACT.Exp, bias=neg_m[:])
+        pv_bf0 = interleave("pv0", pv0_raw, True)
+        pv_bf1 = interleave("pv1", pv1_raw, False)
         r = column("r")
+        late = sbuf("late", [P, P + G + 16], tag="pv1")
+        sums_t, mo_s = late[:, :P], late[:, P:P + G]
+        neg_gain, neg_r = late[:, P + G:P + G + 1], late[:, P + G + 8:P + G + 9]
         nc.vector.reciprocal(r[:], z[:])
-        c0_ps = ps.tile([P, U], F32, name="c0_ps")
-        c0_b_ps = ps.tile([P, HALF], F32, name="c0_b_ps")
-        c0 = sbuf("c0", [P, U])
-        quantize(pv_bf0, pv, halves[0])
-        product(c0_ps[:, halves[0]], go, pv, halves[0], FP8X4)
-        nc.scalar.copy(out=c0[:, halves[0]], in_=c0_ps[:, halves[0]])
-        quantize(pv_bf1, pv, halves[1])
-        product(c0_b_ps[:], go, pv, halves[1], FP8X4)
-        product(c0_ps[:, halves[1]], go, pv, halves[1], FP8X4)
-        nc.scalar.copy(out=c0[:, halves[1]], in_=c0_b_ps[:])
         xpb = sbuf("xpb", [P, U])
         xz = column("xz")
         nc.vector.scalar_tensor_tensor(out=xpb[:], in0=tb_ps[:], scalar=1.0, in1=pb[:], op0=ALU.mult, op1=ALU.mult,
                                        accum_out=xz[:])
+        quantize(pv_bf0, pv, halves[0])
+        mu = column("mu")
+        nc.vector.tensor_tensor(out=mu[:], in0=xz[:], in1=r[:], op=ALU.mult)
+        quantize(pv_bf1, pv, halves[1])
+        nc.scalar.copy(out=sums_t[:], in_=sums_t_ps[:])
+        sums_ps = ps.tile([P, P], F32, name="sums_ps", tag="c1")
+        nc.tensor.transpose(sums_ps[:], sums_t[:], ident[:])
+        c0_a_ps = ps.tile([P, HALF], F32, name="c0_a_ps", tag="a")
+        product(c0_a_ps[:], go, pv, halves[0], FP8X4)
+        c0_b_ps = ps.tile([P, HALF], F32, name="c0_b_ps")
+        product(c0_b_ps[:], go, pv, halves[1], FP8X4)
+        nc.scalar.mul(neg_gain[:], r[:], -256.0)
+        nc.scalar.activation(out=mo_s[:], in_=mo[:], func=ACT.Copy, scale=neg_gain[:])
+        c0 = sbuf("c0", [P, U])
+        nc.scalar.copy(out=c0[:, halves[0]], in_=c0_a_ps[:])
+        nc.scalar.copy(out=c0[:, halves[1]], in_=c0_b_ps[:])
+        nc.scalar.mul(neg_r[:], r[:], -1.0)
+        r_gain = column("r_gain")
+        nc.scalar.activation(out=r_gain[:], in_=r[:], func=ACT.Copy, scale=neg_gain[:])
+        slope = sbuf("slope", [P, U], tag="pv1_bf")
+        nc.vector.scalar_tensor_tensor(out=slope[:], in0=tb_ps[:], scalar=mu[:], in1=pb[:], op0=ALU.subtract,
+                                       op1=ALU.mult)
         rs = sbuf("rs", [P, G])
         nc.vector.reciprocal(rs[:], sums_ps[:, :G])
-        tb_g = sbuf("tb_g", [P, G])
-        nc.vector.tensor_copy(tb_g[:], tb[:].indirect(opened[:]))
-        hh = sbuf("hh", [P, G])
-        nc.vector.tensor_tensor(out=hh[:], in0=sums_ps[:, G:], in1=rs[:], op=ALU.mult)
-
-        neg_gain = column("neg_gain")
-        neg_r = column("neg_r")
-        r_gain = column("r_gain")
-        mu = column("mu")
-        mo = sbuf("mo", [P, G])
-        mo_s = sbuf("mo_s", [P, G])
-        nc.scalar.mul(neg_gain[:], r[:], -256.0)
-        nc.scalar.activation(out=mo[:], in_=b_g[:], func=ACT.Exp, bias=neg_m[:])
-        nc.scalar.activation(out=mu[:], in_=xz[:], func=ACT.Copy, scale=r[:])
-        nc.scalar.activation(out=mo_s[:], in_=mo[:], func=ACT.Copy, scale=neg_gain[:])
-        nc.scalar.mul(neg_r[:], r[:], -1.0)
-        nc.scalar.activation(out=r_gain[:], in_=r[:], func=ACT.Copy, scale=neg_gain[:])
-
         slope_g = sbuf("slope_g", [P, G])
         nc.vector.scalar_tensor_tensor(out=slope_g[:], in0=tb_g[:], scalar=mu[:], in1=mo_s[:], op0=ALU.subtract,
                                        op1=ALU.mult)
+        hh = sbuf("hh", [P, G])
+        nc.vector.tensor_tensor(out=hh[:], in0=sums_ps[:, G:], in1=rs[:], op=ALU.mult)
         nd = sbuf("nd", [P, G])
         nc.vector.tensor_tensor(out=nd[:], in0=c0[:].indirect(opened[:]), in1=hh[:], op=ALU.subtract)
-        y = sbuf("y", [P, U])
+        y = sbuf("y", [P, U], tag="rs")
         n0 = column("n0")
+        nc.vector.scalar_tensor_tensor(out=y[:], in0=c0[:], scalar=1.0, in1=pb[:], op0=ALU.mult, op1=ALU.mult,
+                                       accum_out=n0[:])
         j1 = sbuf("j1", [P, G])
-        n1 = column("n1")
+        n1 = column("n1", tag="n1")
         nc.vector.scalar_tensor_tensor(out=j1[:], in0=nd[:], scalar=1.0 / 256.0, in1=mo_s[:], op0=ALU.mult,
                                        op1=ALU.mult, accum_out=n1[:])
         nc.vector.tensor_tensor(out=xs[:].indirect(opened[:]), in0=nd[:], in1=slope_g[:], op=ALU.mult)
-        nc.vector.scalar_tensor_tensor(out=y[:], in0=c0_ps[:], scalar=1.0, in1=pb[:], op0=ALU.mult, op1=ALU.mult,
-                                       accum_out=n0[:])
-        bx = sbuf("bx", [P, U])
-        nc.gpsimd.tensor_tensor(out=bx[:], in0=xs[:], in1=base_sb[:], op=ALU.add)
-        j2 = sbuf("j2", [P, U])
-        k1 = column("k1")
-        nc.scalar.activation(out=j2[:], in_=xs[:], func=ACT.Copy, scale=neg_r[:], accum_out=k1[:])
         n = column("n")
         nc.scalar.activation(out=n[:], in_=n0[:], func=ACT.Identity, scale=r[:], bias=n1[:])
-        slope = sbuf("slope", [P, U])
-        nc.vector.scalar_tensor_tensor(out=slope[:], in0=tb_ps[:], scalar=mu[:], in1=pb[:], op0=ALU.subtract,
-                                       op1=ALU.mult)
+        j2 = sbuf("j2", [P, U], tag="n1")
+        k1 = column("k1")
+        nc.scalar.activation(out=j2[:], in_=xs[:], func=ACT.Copy, scale=neg_r[:], accum_out=k1[:])
+        bx = sbuf("bx", [P, U])
+        nc.vector.tensor_tensor(out=bx[:, halves[0]], in0=xs[:, halves[0]], in1=base_sb[:, halves[0]], op=ALU.add)
         u = sbuf("u", [P, U])
         k0 = column("k0")
-        nc.vector.scalar_tensor_tensor(out=u[:], in0=c0_ps[:], scalar=n[:], in1=slope[:], op0=ALU.subtract,
+        nc.vector.scalar_tensor_tensor(out=u[:], in0=c0[:], scalar=n[:], in1=slope[:], op0=ALU.subtract,
                                        op1=ALU.mult, accum_out=k0[:])
+        nc.vector.tensor_tensor(out=bx[:, halves[1]], in0=xs[:, halves[1]], in1=base_sb[:, halves[1]], op=ALU.add)
         shift = column("shift")
         nc.scalar.activation(out=shift[:], in_=k0[:], func=ACT.Identity, scale=r_gain[:], bias=k1[:])
         w = [sbuf("w%d" % h, [P, HALF]) for h in range(2)]

from contextlib import ExitStack

import concourse.mybir as mybir
from concourse.masks import make_identity

D, E, U, T, I, G, Q = 512, 512, 512, 2048, 512, 64, 128
FLOPS = 2 * 512 * 128 * 512 * 5

F32 = mybir.dt.float32
BF16 = mybir.dt.bfloat16
I32 = mybir.dt.int32
U32 = mybir.dt.uint32
U16 = mybir.dt.uint16
U8 = mybir.dt.uint8
FP8X4 = mybir.dt.float8_e4m3fn_x4
FP4X4 = mybir.dt.float4_e2m1fn_x4
ALU = mybir.AluOpType
ACT = mybir.ActivationFunctionType
AXIS = mybir.AxisListType

P = 128
PACK = 4
HALF = U // 2
PAGE = I // G


def tile_attend_hvopened_b_kernel(tc, pquery, pgsum, query, keys_words, keys_scales, gout, pvals,
                                   vals_words, vals_scales, dpquery, base, offs, offs2, out):
    nc = tc.nc
    with ExitStack() as ctx:
        sb = ctx.enter_context(tc.tile_pool(name="sb", bufs=1))
        ps = ctx.enter_context(tc.psum_pool(name="ps", bufs=1))

        def sbuf(name, shape, dtype=F32, tag=None):
            return sb.tile(shape, dtype, name=name, tag=tag or name, align_bytes=64)

        def column(name, tag=None):
            return sbuf(name, [P, 1], tag=tag)

        def load_rows(name, src, cols, queue, tag=None):
            raw = sbuf(name + "_raw", [P, PACK, cols.stop - cols.start], tag=tag)
            queue.dma_start(out=raw[:], in_=src.rearrange("(p j) w -> p j w", j=PACK)[:, :, cols])
            return raw

        def interleave(name, raw, on_vector, tag=None):
            width = raw.shape[2]
            grouped = sbuf(name + "_bf", [P, width, PACK], BF16, tag=tag)
            dst = grouped[:].rearrange("p (c i) t -> p c t i", i=4)
            src = raw[:].rearrange("p t (c i) -> p c t i", i=4)
            if on_vector:
                nc.vector.tensor_copy(out=dst, in_=src)
            else:
                nc.scalar.copy(out=dst, in_=src)
            return grouped

        def planes(name, width, tag=None):
            return sbuf(name + "_codes", [P, width], U32, tag=tag), sbuf(name + "_scales", [P, width], U8)

        def quantize(grouped, operand, cols):
            codes, scales = operand
            nc.vector.quantize_mx(out=codes[:, cols].bitcast(FP8X4), scales=scales[:, cols],
                                  in_=grouped[:].rearrange("p w j -> p (w j)"))

        def product(acc, rows, moving, cols, fmt):
            nc.tensor.matmul_mx(out=acc, lhsT=rows[0][:].bitcast(FP8X4), lhsT_scale=rows[1][:],
                                rhs=moving[0][:, cols].bitcast(fmt), rhs_scale=moving[1][:, cols],
                                start=True, stop=True)

        def load_scale_rows(tile, src, queue):
            for r in range(4):
                queue.dma_start(out=tile[r:P:32, :].bitcast(I32), in_=src[0][r:16:4, :].bitcast(I32))

        rows_q = slice(0, Q)
        whole = slice(0, U)
        halves = [slice(0, HALF), slice(HALF, U)]

        slots = sb.tile([P, I // 16], U16, name="slots")
        opened = sb.tile([P, G // 16], U16, name="opened")
        kw = sbuf("kw", [P, T], U16)
        vw = sbuf("vw", [P, T], U16)
        ks = sbuf("ks", [P, T], U8)
        vs = sbuf("vs", [P, T], U8)
        xs = sbuf("xs", [P, U])
        ident = sbuf("ident", [P, P])
        warm = column("warm")
        warm2 = column("warm2")
        nc.gpsimd.memset(ks[:].bitcast(I32), 0)
        nc.vector.memset(warm[:], 0.0)
        nc.vector.memset(vs[:].bitcast(I32), 0)
        nc.scalar.activation(out=warm2[:], in_=warm[:], func=ACT.Exp)
        nc.sync.dma_start(slots[:], offs)
        nc.sync.dma_start(out=kw[:].bitcast(I32), in_=keys_words[0].bitcast(I32))
        load_scale_rows(ks, keys_scales, nc.sync)
        q_raw = load_rows("q", query, rows_q, nc.sync)
        pg0_raw = load_rows("pg0", pgsum, halves[0], nc.sync)
        pq_raw = load_rows("pq", pquery, rows_q, nc.sync)
        load_scale_rows(vs, vals_scales, nc.sync)
        pg1_raw = load_rows("pg1", pgsum, halves[1], nc.sync, "pg1")
        dq_raw = load_rows("dq", dpquery, rows_q, nc.sync)
        go_raw = load_rows("go", gout, rows_q, nc.sync)
        nc.sync.dma_start(out=vw[:].bitcast(I32), in_=vals_words[0].bitcast(I32))
        nc.sync.dma_start(opened[:], offs2)
        pv0_raw = load_rows("pv0", pvals, halves[0], nc.sync, "pv0")
        pv1_raw = load_rows("pv1", pvals, halves[1], nc.sync, "pv1")
        base_sb = sbuf("base_sb", [P, U])
        nc.sync.dma_start(out=base_sb[:], in_=base)
        make_identity(nc, ident[:])
        nc.gpsimd.memset(xs[:], 0.0)
        keys = (sbuf("keys_w", [P, I], U16), sbuf("keys_s", [P, I], U8))
        vals = (sbuf("vals_w", [P, I], U16), sbuf("vals_s", [P, I], U8))
        dq = planes("dq", Q)
        qq = planes("qq", Q)
        go = planes("go", Q)
        page_planes = planes("pg", U + Q, "pg1")
        pg = [x[:, :U] for x in page_planes]
        pq = [x[:, U:] for x in page_planes]
        pv = planes("pv", U)
        nc.vector.tensor_copy(keys[0][:], kw[:].indirect(slots[:]))
        nc.vector.tensor_copy(keys[1][:], ks[:].indirect(slots[:]))
        q_bf = interleave("q", q_raw, False)
        pg_bf0 = interleave("pg0", pg0_raw, False)
        pq_bf = interleave("pq", pq_raw, False)
        quantize(q_bf, qq, rows_q)
        a_ps = ps.tile([P, I], F32, name="a_ps", tag="a")
        product(a_ps[:], qq, keys, whole, FP4X4)
        nc.vector.tensor_copy(vals[1][:], vs[:].indirect(slots[:]))
        terms = sbuf("terms", [P, PAGE, 2 * G])
        nc.scalar.activation(out=terms[:, :, :G], in_=a_ps[:].rearrange("p (g j) -> p j g", j=PAGE), func=ACT.Exp)
        pg_bf1 = interleave("pg1", pg1_raw, True)
        dq_bf = interleave("dq", dq_raw, False)
        go_bf = interleave("go", go_raw, False)
        quantize(pg_bf0, pg, halves[0])
        quantize(pq_bf, pq, rows_q)
        quantize(pg_bf1, pg, halves[1])
        b_ps = ps.tile([P, U], F32, name="b_ps")
        product(b_ps[:], pq, pg, whole, FP8X4)
        quantize(dq_bf, dq, rows_q)
        tb_ps = ps.tile([P, U], F32, name="tb_ps")
        product(tb_ps[:], dq, pg, whole, FP8X4)
        quantize(go_bf, go, rows_q)
        nc.vector.tensor_copy(vals[0][:], vw[:].indirect(slots[:]))
        c1_ps = ps.tile([P, I], F32, name="c1_ps", tag="c1")
        product(c1_ps[:], go, vals, whole, FP4X4)
        b = sbuf("b", [P, U])
        nc.scalar.copy(out=b[:], in_=b_ps[:])
        tb = sbuf("tb", [P, U])
        nc.scalar.copy(out=tb[:], in_=tb_ps[:])
        neg_m = column("neg_m")
        nc.vector.tensor_reduce(out=neg_m[:], in_=b_ps[:], axis=AXIS.X, op=ALU.max, negate=True)
        b_g = sbuf("b_g", [P, G])
        nc.vector.tensor_copy(b_g[:], b[:].indirect(opened[:]))
        tb_g = sbuf("tb_g", [P, G])
        nc.vector.tensor_copy(tb_g[:], tb[:].indirect(opened[:]))
        sums_t_ps = ps.tile([P, P], F32, name="sums_t_ps", tag="a")
        for part in range(2):
            places = slice(part * PAGE // 2, (part + 1) * PAGE // 2)
            nc.vector.tensor_tensor(out=terms[:, places, G:],
                                    in0=c1_ps[:].rearrange("p (g j) -> p j g", j=PAGE)[:, places, :],
                                    in1=terms[:, places, :G], op=ALU.mult)
            for j in range(places.start, places.stop):
                nc.tensor.matmul(sums_t_ps[:], lhsT=terms[:, j, :], rhs=ident[:], is_transpose=True,
                                 start=(j == 0), stop=(j == PAGE - 1))
        pb = sbuf("pb", [P, U])
        z = column("z")
        nc.scalar.activation(out=pb[:], in_=b[:], func=ACT.Exp, bias=neg_m[:], accum_out=z[:])
        mo = sbuf("mo", [P, G])
        nc.scalar.activation(out=mo[:], in_=b_g[:], func=ACT.Exp, bias=neg_m[:])
        pv_bf0 = interleave("pv0", pv0_raw, True)
        pv_bf1 = interleave("pv1", pv1_raw, False)
        r = column("r")
        late = sbuf("late", [P, P + G + 16], tag="pv1")
        sums_t, mo_s = late[:, :P], late[:, P:P + G]
        neg_gain, neg_r = late[:, P + G:P + G + 1], late[:, P + G + 8:P + G + 9]
        nc.vector.reciprocal(r[:], z[:])
        xpb = sbuf("xpb", [P, U])
        xz = column("xz")
        nc.vector.scalar_tensor_tensor(out=xpb[:], in0=tb_ps[:], scalar=1.0, in1=pb[:], op0=ALU.mult, op1=ALU.mult,
                                       accum_out=xz[:])
        quantize(pv_bf0, pv, halves[0])
        mu = column("mu")
        nc.vector.tensor_tensor(out=mu[:], in0=xz[:], in1=r[:], op=ALU.mult)
        quantize(pv_bf1, pv, halves[1])
        nc.scalar.copy(out=sums_t[:], in_=sums_t_ps[:])
        sums_ps = ps.tile([P, P], F32, name="sums_ps", tag="c1")
        nc.tensor.transpose(sums_ps[:], sums_t[:], ident[:])
        c0_a_ps = ps.tile([P, HALF], F32, name="c0_a_ps", tag="a")
        product(c0_a_ps[:], go, pv, halves[0], FP8X4)
        c0_b_ps = ps.tile([P, HALF], F32, name="c0_b_ps")
        product(c0_b_ps[:], go, pv, halves[1], FP8X4)
        nc.scalar.mul(neg_gain[:], r[:], -256.0)
        nc.scalar.activation(out=mo_s[:], in_=mo[:], func=ACT.Copy, scale=neg_gain[:])
        c0 = sbuf("c0", [P, U])
        nc.scalar.copy(out=c0[:, halves[0]], in_=c0_a_ps[:])
        nc.scalar.copy(out=c0[:, halves[1]], in_=c0_b_ps[:])
        nc.scalar.mul(neg_r[:], r[:], -1.0)
        r_gain = column("r_gain")
        nc.scalar.activation(out=r_gain[:], in_=r[:], func=ACT.Copy, scale=neg_gain[:])
        slope = sbuf("slope", [P, U], tag="pv1_bf")
        nc.vector.scalar_tensor_tensor(out=slope[:], in0=tb_ps[:], scalar=mu[:], in1=pb[:], op0=ALU.subtract,
                                       op1=ALU.mult)
        rs = sbuf("rs", [P, G])
        nc.vector.reciprocal(rs[:], sums_ps[:, :G])
        slope_g = sbuf("slope_g", [P, G])
        nc.vector.scalar_tensor_tensor(out=slope_g[:], in0=tb_g[:], scalar=mu[:], in1=mo_s[:], op0=ALU.subtract,
                                       op1=ALU.mult)
        hh = sbuf("hh", [P, G])
        nc.vector.tensor_tensor(out=hh[:], in0=sums_ps[:, G:], in1=rs[:], op=ALU.mult)
        nd = sbuf("nd", [P, G])
        nc.vector.tensor_tensor(out=nd[:], in0=c0[:].indirect(opened[:]), in1=hh[:], op=ALU.subtract)
        y = sbuf("y", [P, U], tag="rs")
        n0 = column("n0")
        nc.vector.scalar_tensor_tensor(out=y[:], in0=c0[:], scalar=1.0, in1=pb[:], op0=ALU.mult, op1=ALU.mult,
                                       accum_out=n0[:])
        j1 = sbuf("j1", [P, G])
        n1 = column("n1", tag="n1")
        nc.vector.scalar_tensor_tensor(out=j1[:], in0=nd[:], scalar=1.0 / 256.0, in1=mo_s[:], op0=ALU.mult,
                                       op1=ALU.mult, accum_out=n1[:])
        nc.vector.tensor_tensor(out=xs[:].indirect(opened[:]), in0=nd[:], in1=slope_g[:], op=ALU.mult)
        n = column("n")
        nc.scalar.activation(out=n[:], in_=n0[:], func=ACT.Identity, scale=r[:], bias=n1[:])
        j2 = sbuf("j2", [P, U], tag="n1")
        k1 = column("k1")
        nc.scalar.activation(out=j2[:], in_=xs[:], func=ACT.Copy, scale=neg_r[:], accum_out=k1[:])
        bx = sbuf("bx", [P, U])
        nc.vector.tensor_tensor(out=bx[:, halves[0]], in0=xs[:, halves[0]], in1=base_sb[:, halves[0]], op=ALU.add)
        u = sbuf("u", [P, U])
        k0 = column("k0")
        nc.vector.scalar_tensor_tensor(out=u[:], in0=c0[:], scalar=n[:], in1=slope[:], op0=ALU.subtract,
                                       op1=ALU.mult, accum_out=k0[:])
        nc.vector.tensor_tensor(out=bx[:, halves[1]], in0=xs[:, halves[1]], in1=base_sb[:, halves[1]], op=ALU.add)
        shift = column("shift")
        nc.scalar.activation(out=shift[:], in_=k0[:], func=ACT.Identity, scale=r_gain[:], bias=k1[:])
        w = [sbuf("w%d" % h, [P, HALF]) for h in range(2)]
        result = [sbuf("result%d" % h, [P, HALF]) for h in range(2)]
        for h in range(2):
            nc.vector.scalar_tensor_tensor(out=w[h][:], in0=u[:, halves[h]], scalar=neg_gain[:],
                                           in1=bx[:, halves[h]], op0=ALU.mult, op1=ALU.subtract)
        for h in range(2):
            nc.vector.scalar_tensor_tensor(out=result[h][:], in0=pb[:, halves[h]], scalar=shift[:],
                                           in1=w[h][:], op0=ALU.mult, op1=ALU.subtract)
            nc.sync.dma_start(out=out[:, halves[h]], in_=result[h][:])
